import numpy as np
import ml_dtypes


def mxq(x, axis, fmt="e4m3"):
    dtype, down = {"e4m3": (ml_dtypes.float8_e4m3fn, 7), "e5m2": (ml_dtypes.float8_e5m2, 14)}[fmt]
    v = np.moveaxis(np.asarray(x, np.float32).astype(ml_dtypes.bfloat16).astype(np.float64), axis, -1)
    blocks = v.reshape(v.shape[:-1] + (-1, 32))
    amax = np.abs(blocks).max(-1, keepdims=True)
    byte = np.maximum(np.where(amax > 0, np.frexp(amax)[1] - 1 + 127, 0) - down, 1)
    scale = np.exp2(byte - 127.0)
    codes = (blocks / scale).astype(np.float32).astype(dtype).astype(np.float64)
    return np.moveaxis((codes * scale).reshape(v.shape), -1, axis)


WIDE = False


def mx_kscale(k):
    if not WIDE:
        return np.ones(k)
    levels = np.array([10, -10, 5, -5, 0])
    if k % 512:
        return np.exp2(np.random.permutation(np.resize(levels, k // 32))).repeat(32)
    a = np.empty((k // 512, 16))
    for p in range(k // 512):
        a[p, :8] = np.random.permutation(np.resize(levels, 8))
        for g in range(8):
            far = levels[np.abs(levels - a[p, g]) >= 10]
            a[p, g + 8] = far[np.random.randint(len(far))]
    return np.exp2(a.ravel()).repeat(32)


def f64(x):
    return np.asarray(x).astype(np.float64)


def striped(idx):
    return np.tile(idx.reshape(-1, 16).T, (8, 1)).astype(np.uint16)


def unstriped(offs):
    return offs[:16].T.reshape(-1).astype(np.int64)


def striped8(idx):
    return np.concatenate([x.reshape(-1, 16).T for x in idx]).astype(np.uint16)


def runs(offs, k):
    lists = np.stack([offs[16 * r : 16 * r + 16].T.reshape(-1) for r in range(8)]).astype(np.int64)
    return lists[np.arange(k) % 512 // 64]


def pack_weight(w):
    k, n = w.shape
    w = f64(np.asarray(w, np.float32).astype(ml_dtypes.bfloat16)).reshape(k // 32, 32, n)
    amax = np.abs(w).max(1)
    byte = np.clip(np.where(amax > 0, np.frexp(amax)[1] - 1 + 127 - 7, 1), 1, 254)
    scaled = (w * np.exp2(127.0 - byte)[:, None, :]).reshape(k, n).astype(np.float32)
    words = np.ascontiguousarray(scaled.reshape(k // 512, 128, 4, n).transpose(0, 1, 3, 2)).astype(ml_dtypes.float8_e4m3fn).view(np.uint8)
    return words, np.ascontiguousarray(byte.astype(np.uint8).reshape(k // 512, 16, n))


def unpack_weight(words, scales):
    g, p, n, _ = words.shape
    vals = np.ascontiguousarray(words).view(ml_dtypes.float8_e4m3fn).astype(np.float64) * np.repeat(np.exp2(scales.astype(np.float64) - 127.0), 8, axis=1)[..., None]
    return vals.transpose(0, 1, 3, 2).reshape(g * 512, n)


E2M1 = np.array([0.0, 0.5, 1.0, 1.5, 2.0, 3.0, 4.0, 6.0, -0.0, -0.5, -1.0, -1.5, -2.0, -3.0, -4.0, -6.0])


def pack_fp4(w):
    k, n = w.shape
    w = f64(np.asarray(w, np.float32).astype(ml_dtypes.bfloat16)).reshape(k // 32, 32, n)
    amax = np.abs(w).max(1)
    mant, ex = np.frexp(amax / 6.0)
    byte = np.clip(np.where(amax > 0, np.where(mant > 0.5, ex, ex - 1) + 127, 1), 1, 254)
    scaled = (w * np.exp2(127.0 - byte)[:, None, :]).reshape(k, n).astype(np.float32)
    c = np.ascontiguousarray(scaled.reshape(k // 512, 128, 4, n).transpose(0, 1, 3, 2)).astype(ml_dtypes.float4_e2m1fn).view(np.uint8) & 0xF
    words = (c[..., 0::2] | (c[..., 1::2] << 4)).reshape(k // 512, 128, 2 * n)
    return np.ascontiguousarray(words), np.ascontiguousarray(byte.astype(np.uint8).reshape(k // 512, 16, n))


def unpack_fp4(words, scales):
    g, _, n = scales.shape
    words = np.ascontiguousarray(words).reshape(g, 128, n, 2)
    nib = np.empty((g, 128, n, 4), np.uint8)
    nib[..., 0::2] = words & 0xF
    nib[..., 1::2] = words >> 4
    vals = E2M1[nib] * np.repeat(np.exp2(scales.astype(np.float64) - 127.0), 8, axis=1)[..., None]
    return vals.transpose(0, 1, 3, 2).reshape(g * 512, n)


def silu(v):
    return v / (1.0 + np.exp(-np.maximum(v, -700.0)))

def planes(y):
    n, m = y.shape
    v = y.astype(np.float32).astype(ml_dtypes.bfloat16).astype(np.float64).reshape(n // 32, 32, m)
    top = np.abs(v).max(1)
    byte = np.clip(np.where(top > 0, np.frexp(top)[1] - 1 + 127 - 7, 1), 1, 254)
    codes = (v * np.exp2(127.0 - byte)[:, None, :]).reshape(n, m).astype(np.float32).astype(ml_dtypes.float8_e4m3fn).view(np.uint8)
    words = codes.reshape(n // 512, 128, 4, m).transpose(0, 1, 3, 2)
    return np.ascontiguousarray(words), np.ascontiguousarray(byte.astype(np.uint8).reshape(n // 512, 16, m))


K, T, S, V, N, H = 512, 2048, 512, 256, 512, 512


def setup_inputs():
    n = np.random.standard_normal
    s = mx_kscale(K)[:, None]
    u = mx_kscale(S)
    packed_xT = pack_weight(n((K, T)) * s)
    packed_w1 = pack_fp4(n((S, N)) / np.sqrt(S) / u[:, None])
    return {
        "x_words": packed_xT[0],
        "x_scales": packed_xT[1],
        "wa": (n((K, H)) / np.sqrt(K) / s).astype(np.float32),
        "gt": (np.random.uniform(0.5, 1.5, (S, 1)) * u[:, None]).astype(np.float32),
        "w1_words": packed_w1[0],
        "w1_scales": packed_w1[1],
        "offs": striped(np.random.permutation(T)[:S]),
        "fl": striped8(np.stack([np.random.permutation(H)[:V] for _ in range(8)])),
    }


def reference(x_words, x_scales, wa, gt, w1_words, w1_scales, offs, fl):
    xq = unpack_weight(x_words, x_scales)[:, unstriped(offs)]
    y = xq.T @ mxq(f64(wa), 0, "e4m3")
    z = f64(gt) * (silu(y[np.arange(S)[:, None], runs(fl, S)]))
    out_0 = unpack_fp4(w1_words, w1_scales).T @ mxq(z, 0, "e4m3")
    return (out_0,) + planes(out_0)

@@ -1,0 +1,197 @@
+from contextlib import ExitStack
+
+import concourse.mybir as mybir
+
+K, T, S, V, N, H = 512, 2048, 512, 256, 512, 512
+FLOPS = 2 * K * S * H + 2 * S * N * V
+
+F32 = mybir.dt.float32
+BF16 = mybir.dt.bfloat16
+I32 = mybir.dt.int32
+U32 = mybir.dt.uint32
+U16 = mybir.dt.uint16
+U8 = mybir.dt.uint8
+FP8X4 = mybir.dt.float8_e4m3fn_x4
+FP4X4 = mybir.dt.float4_e2m1fn_x4
+SILU = mybir.ActivationFunctionType.Silu
+MULT = mybir.AluOpType.mult
+
+P = 128
+PACK = 4
+EARLY = 384
+HALF = V // 2
+
+
+def interleave(copy, dst, src):
+    copy(out=dst.rearrange("p (c i) t -> p c t i", i=4), in_=src.rearrange("p t (c i) -> p c t i", i=4))
+
+
+def quantize(nc, codes, scales, grouped):
+    nc.vector.quantize_mx(out=codes.bitcast(FP8X4), scales=scales, in_=grouped.rearrange("p c t -> p (c t)"))
+
+
+def tile_picked_tokmixl_silu_po_kernel(
+    tc, x_words, x_scales, wa, gt, w1_words, w1_scales, offs, fl, out_0, out_1, out_2
+):
+    nc = tc.nc
+    with ExitStack() as ctx:
+        sb = ctx.enter_context(tc.tile_pool(name="sb", bufs=1))
+        shared = ctx.enter_context(tc.tile_pool(name="shared", bufs=1))
+        psum = ctx.enter_context(tc.psum_pool(name="psum", bufs=8))
+
+        offs_sb = sb.tile([P, S // 16], U16, name="offs_sb")
+        fl_sb = sb.tile([P, V // 16], U16, name="fl_sb")
+        xw = shared.tile([P, T], I32, name="xw", align_bytes=64, offset=0)
+        xs = sb.tile([P, T], U8, name="xs", align_bytes=64)
+        wa_early = sb.tile([P, PACK, EARLY], F32, name="wa_early", align_bytes=64)
+        wa_late = sb.tile([P, PACK, H - EARLY], F32, name="wa_late", align_bytes=64)
+        w1w = sb.tile([P, 2 * N], U8, name="w1w", align_bytes=64)
+        w1s = sb.tile([P, N], U8, name="w1s", align_bytes=64)
+        gt_sb = sb.tile([P, PACK], F32, name="gt_sb", align_bytes=64)
+        warm_in = sb.tile([P, 1], F32, name="warm_in")
+        warm_out = sb.tile([P, 1], F32, name="warm_out")
+
+        wa_rows = wa.rearrange("(p j) c -> p j c", j=PACK)
+
+        nc.vector.memset(xs[:].bitcast(I32), 0)
+        nc.vector.memset(warm_in[:], 0.0)
+        nc.gpsimd.memset(w1s[:].bitcast(I32), 0)
+
+        nc.sync.dma_start(out=gt_sb[:], in_=gt.rearrange("(p t) o -> p (t o)", t=PACK))
+        nc.sync.dma_start(out=wa_early[:], in_=wa_rows[:, :, 0:EARLY])
+        nc.sync.dma_start(offs_sb[:], offs)
+        for q in range(4):
+            nc.sync.dma_start(
+                out=xs[32 * q : 32 * q + 4, :].bitcast(I32), in_=x_scales[0, 4 * q : 4 * q + 4, :].bitcast(I32)
+            )
+        nc.sync.dma_start(out=xw[:], in_=x_words[0].rearrange("p n t -> p (n t)").bitcast(I32))
+        nc.sync.dma_start(out=wa_late[:], in_=wa_rows[:, :, EARLY:H])
+        nc.sync.dma_start(out=w1w[:].bitcast(I32), in_=w1_words[0].bitcast(I32))
+        nc.sync.dma_start(fl_sb[:], fl)
+        for q in range(4):
+            nc.sync.dma_start(
+                out=w1s[32 * q : 32 * q + 4, :].bitcast(I32), in_=w1_scales[0, 4 * q : 4 * q + 4, :].bitcast(I32)
+            )
+
+        nc.scalar.activation(out=warm_out[:], in_=warm_in[:], func=SILU)
+
+        gtb = sb.tile([P, PACK, V], F32, name="gtb", align_bytes=64)
+        nc.vector.tensor_copy(out=gtb[:], in_=gt_sb[:].unsqueeze(2).to_broadcast([P, PACK, V]))
+
+        xsg = sb.tile([P, S], U8, name="xsg", align_bytes=64)
+        xsd = sb.tile([P, S], U8, name="xsd", align_bytes=64)
+        nc.vector.tensor_copy(out=xsg[:], in_=xs[:].indirect(offs_sb[:]))
+
+        wc = sb.tile([P, EARLY], I32, name="wc", align_bytes=64)
+        ws = sb.tile([P, EARLY], U8, name="ws", align_bytes=64)
+        wb0 = sb.tile([P, 256, PACK], BF16, name="wb0", align_bytes=64)
+        wb1 = sb.tile([P, 128, PACK], BF16, name="wb1", align_bytes=64)
+        wb2 = sb.tile([P, 128, PACK], BF16, name="wb2", align_bytes=64)
+        interleave(nc.scalar.copy, wb0[:], wa_early[:, :, 0:256])
+        interleave(nc.vector.tensor_copy, wb1[:], wa_early[:, :, 256:384])
+        nc.vector.tensor_copy(
+            out=xsd[:].rearrange("p (t s) -> p t s", t=PACK), in_=xsg[:].rearrange("p (s t) -> p t s", t=PACK)
+        )
+        quantize(nc, wc[:, 256:384], ws[:, 256:384], wb1[:])
+        quantize(nc, wc[:, 0:256], ws[:, 0:256], wb0[:])
+
+        xg = sb.tile([P, S], I32, name="xg", align_bytes=64)
+        nc.vector.tensor_copy(
+            out=xg[:].bitcast(U32).rearrange("p (t s) -> p s t", t=PACK),
+            in_=xw[:].bitcast(U32).indirect(offs_sb[:]),
+        )
+        interleave(nc.scalar.copy, wb2[:], wa_late[:])
+        wc2 = shared.tile([P, H - EARLY], I32, name="wc2", align_bytes=64, offset=0)
+        ws2 = shared.tile([P, H - EARLY], U8, name="ws2", align_bytes=64, offset=512)
+        quantize(nc, wc2[:], ws2[:], wb2[:])
+        w1d = shared.tile([P, 2 * N], U8, name="w1d", align_bytes=64, offset=1024)
+        nc.vector.tensor_copy(
+            out=w1d[:].rearrange("p (t s b) -> p t s b", t=PACK, b=2),
+            in_=w1w[:].rearrange("p (s t b) -> p t s b", t=PACK, b=2),
+        )
+
+        w1sd = shared.tile([P, N], U8, name="w1sd", align_bytes=64, offset=2048)
+        nc.vector.tensor_copy(
+            out=w1sd[:].rearrange("p (t s) -> p t s", t=PACK), in_=w1s[:].rearrange("p (s t) -> p t s", t=PACK)
+        )
+
+        def first_product(acc, t, codes, scales):
+            nc.tensor.matmul_mx(
+                out=acc,
+                lhsT=xg[:, P * t : P * (t + 1)].bitcast(FP8X4),
+                lhsT_scale=xsd[:, P * t : P * (t + 1)],
+                rhs=codes.bitcast(FP8X4),
+                rhs_scale=scales,
+                start=True,
+                stop=True,
+            )
+
+        g = sb.tile([P, PACK, V], F32, name="g", align_bytes=64)
+        for t in range(PACK):
+            act = sb.tile([P, H], F32, name="act%d" % t, align_bytes=64)
+            if t == 0:
+                ya = psum.tile([P, EARLY], F32, name="ya", tag="bank")
+                yb = psum.tile([P, H - EARLY], F32, name="yb", tag="bank")
+                first_product(ya[:, 0:256], t, wc[:, 0:256], ws[:, 0:256])
+                first_product(ya[:, 256:EARLY], t, wc[:, 256:EARLY], ws[:, 256:EARLY])
+                first_product(yb[:], t, wc2[:], ws2[:])
+                nc.scalar.activation(out=act[:, 0:EARLY], in_=ya[:], func=SILU)
+                nc.scalar.activation(out=act[:, EARLY:H], in_=yb[:], func=SILU)
+            else:
+                y = psum.tile([P, H], F32, name="y", tag="bank")
+                first_product(y[:, 0:256], t, wc[:, 0:256], ws[:, 0:256])
+                first_product(y[:, 256:EARLY], t, wc[:, 256:EARLY], ws[:, 256:EARLY])
+                first_product(y[:, EARLY:H], t, wc2[:], ws2[:])
+                nc.scalar.activation(out=act[:], in_=y[:], func=SILU)
+            if t < PACK - 1:
+                nc.vector.tensor_tensor(out=g[:, t, :], in0=act[:].indirect(fl_sb[:]), in1=gtb[:, t, :], op=MULT)
+            else:
+                for h in range(2):
+                    cols = slice(HALF * h, HALF * (h + 1))
+                    nc.vector.tensor_tensor(
+                        out=g[:, t, cols],
+                        in0=act[:].indirect(fl_sb[:, 8 * h : 8 * h + 8]),
+                        in1=gtb[:, t, cols],
+                        op=MULT,
+                    )
+
+        zb = [sb.tile([P, HALF, PACK], BF16, name="zb%d" % h, align_bytes=64) for h in range(2)]
+        zc = [sb.tile([P, HALF], I32, name="zc%d" % h, align_bytes=64) for h in range(2)]
+        zs = [sb.tile([P, HALF], U8, name="zs%d" % h, align_bytes=64) for h in range(2)]
+        for h in range(2):
+            interleave(nc.vector.tensor_copy, zb[h][:], g[:, :, HALF * h : HALF * (h + 1)])
+        for h in range(2):
+            quantize(nc, zc[h][:], zs[h][:], zb[h][:])
+
+        o32 = sb.tile([P, PACK, V], F32, name="o32", align_bytes=64)
+        ob = [sb.tile([P, HALF, PACK], BF16, name="ob%d" % h, align_bytes=64) for h in range(2)]
+        oc = sb.tile([P, V], I32, name="oc", align_bytes=64)
+        osc = sb.tile([P, V], U8, name="osc", align_bytes=64)
+        out_rows = out_0.rearrange("(p t) v -> p t v", t=PACK)
+        out_words = out_1[0].rearrange("p n t -> p (n t)").bitcast(I32)
+        for h in range(2):
+            cols = slice(HALF * h, HALF * (h + 1))
+            for u in range(2):
+                acc = psum.tile([P, 2, HALF], F32, name="acc", tag="bank")
+                for e in range(2):
+                    t = 2 * u + e
+                    nc.tensor.matmul_mx(
+                        out=acc[:, e, :],
+                        lhsT=w1d[:, 2 * P * t : 2 * P * (t + 1)].bitcast(FP4X4),
+                        lhsT_scale=w1sd[:, P * t : P * (t + 1)],
+                        rhs=zc[h][:].bitcast(FP8X4),
+                        rhs_scale=zs[h][:],
+                        start=True,
+                        stop=True,
+                    )
+                nc.scalar.copy(out=o32[:, 2 * u : 2 * u + 2, cols], in_=acc[:])
+                if h == 1:
+                    nc.sync.dma_start(out=out_rows[:, 2 * u : 2 * u + 2, :], in_=o32[:, 2 * u : 2 * u + 2, :])
+            interleave(nc.vector.tensor_copy, ob[h][:], o32[:, :, cols])
+            quantize(nc, oc[:, cols], osc[:, cols], ob[h][:])
+            nc.sync.dma_start(out=out_words[:, cols], in_=oc[:, cols])
+        for q in range(4):
+            eng = nc.scalar if q < 2 else nc.sync
+            eng.dma_start(
+                out=out_2[0, 4 * q : 4 * q + 4, :].bitcast(I32), in_=osc[32 * q : 32 * q + 4, :].bitcast(I32)
+            )

@@ -43,8 +43,7 @@ def tile_picked_tokmixl_silu_po_kernel(
         fl_sb = sb.tile([P, V // 16], U16, name="fl_sb")
         xw = shared.tile([P, T], I32, name="xw", align_bytes=64, offset=0)
         xs = sb.tile([P, T], U8, name="xs", align_bytes=64)
-        wa_early = sb.tile([P, PACK, EARLY], F32, name="wa_early", align_bytes=64)
-        wa_late = sb.tile([P, PACK, H - EARLY], F32, name="wa_late", align_bytes=64)
+        wa_raw = [sb.tile([P, PACK, 256], F32, name="wa_raw%d" % u, align_bytes=64) for u in range(2)]
         w1w = sb.tile([P, 2 * N], U8, name="w1w", align_bytes=64)
         w1s = sb.tile([P, N], U8, name="w1s", align_bytes=64)
         gt_sb = sb.tile([P, PACK], F32, name="gt_sb", align_bytes=64)
@@ -57,17 +56,17 @@ def tile_picked_tokmixl_silu_po_kernel(
         nc.vector.memset(warm_in[:], 0.0)
         nc.gpsimd.memset(w1s[:].bitcast(I32), 0)
 
-        nc.sync.dma_start(out=gt_sb[:], in_=gt.rearrange("(p t) o -> p (t o)", t=PACK))
-        nc.sync.dma_start(out=wa_early[:], in_=wa_rows[:, :, 0:EARLY])
         nc.sync.dma_start(offs_sb[:], offs)
+        nc.sync.dma_start(out=gt_sb[:], in_=gt.rearrange("(p t) o -> p (t o)", t=PACK))
+        nc.sync.dma_start(fl_sb[:], fl)
         for q in range(4):
             nc.sync.dma_start(
                 out=xs[32 * q : 32 * q + 4, :].bitcast(I32), in_=x_scales[0, 4 * q : 4 * q + 4, :].bitcast(I32)
             )
         nc.sync.dma_start(out=xw[:], in_=x_words[0].rearrange("p n t -> p (n t)").bitcast(I32))
-        nc.sync.dma_start(out=wa_late[:], in_=wa_rows[:, :, EARLY:H])
+        for u in range(2):
+            nc.sync.dma_start(out=wa_raw[u][:], in_=wa_rows[:, :, 256 * u : 256 * (u + 1)])
         nc.sync.dma_start(out=w1w[:].bitcast(I32), in_=w1_words[0].bitcast(I32))
-        nc.sync.dma_start(fl_sb[:], fl)
         for q in range(4):
             nc.sync.dma_start(
                 out=w1s[32 * q : 32 * q + 4, :].bitcast(I32), in_=w1_scales[0, 4 * q : 4 * q + 4, :].bitcast(I32)
@@ -76,90 +75,87 @@ def tile_picked_tokmixl_silu_po_kernel(
         nc.scalar.activation(out=warm_out[:], in_=warm_in[:], func=SILU)
 
         gtb = sb.tile([P, PACK, V], F32, name="gtb", align_bytes=64)
-        nc.vector.tensor_copy(out=gtb[:], in_=gt_sb[:].unsqueeze(2).to_broadcast([P, PACK, V]))
+        nc.scalar.copy(out=gtb[:], in_=gt_sb[:].unsqueeze(2).to_broadcast([P, PACK, V]))
 
         xsg = sb.tile([P, S], U8, name="xsg", align_bytes=64)
         xsd = sb.tile([P, S], U8, name="xsd", align_bytes=64)
         nc.vector.tensor_copy(out=xsg[:], in_=xs[:].indirect(offs_sb[:]))
-
-        wc = sb.tile([P, EARLY], I32, name="wc", align_bytes=64)
-        ws = sb.tile([P, EARLY], U8, name="ws", align_bytes=64)
-        wb0 = sb.tile([P, 256, PACK], BF16, name="wb0", align_bytes=64)
-        wb1 = sb.tile([P, 128, PACK], BF16, name="wb1", align_bytes=64)
-        wb2 = sb.tile([P, 128, PACK], BF16, name="wb2", align_bytes=64)
-        interleave(nc.scalar.copy, wb0[:], wa_early[:, :, 0:256])
-        interleave(nc.vector.tensor_copy, wb1[:], wa_early[:, :, 256:384])
         nc.vector.tensor_copy(
             out=xsd[:].rearrange("p (t s) -> p t s", t=PACK), in_=xsg[:].rearrange("p (s t) -> p t s", t=PACK)
         )
-        quantize(nc, wc[:, 256:384], ws[:, 256:384], wb1[:])
-        quantize(nc, wc[:, 0:256], ws[:, 0:256], wb0[:])
-
         xg = sb.tile([P, S], I32, name="xg", align_bytes=64)
         nc.vector.tensor_copy(
             out=xg[:].bitcast(U32).rearrange("p (t s) -> p s t", t=PACK),
             in_=xw[:].bitcast(U32).indirect(offs_sb[:]),
         )
-        interleave(nc.scalar.copy, wb2[:], wa_late[:])
-        wc2 = shared.tile([P, H - EARLY], I32, name="wc2", align_bytes=64, offset=0)
-        ws2 = shared.tile([P, H - EARLY], U8, name="ws2", align_bytes=64, offset=512)
-        quantize(nc, wc2[:], ws2[:], wb2[:])
+
+        wb = [
+            sb.tile([P, 128, PACK], BF16, name="wb0", align_bytes=64),
+            shared.tile([P, 128, PACK], BF16, name="wb1", align_bytes=64, offset=2048),
+            shared.tile([P, 128, PACK], BF16, name="wb2", align_bytes=64, offset=0),
+            shared.tile([P, 128, PACK], BF16, name="wb3", align_bytes=64, offset=1024),
+        ]
+        wc = [
+            shared.tile([P, 256], I32, name="wc0", align_bytes=64, offset=3072),
+            sb.tile([P, 256], I32, name="wc1", align_bytes=64),
+        ]
+        ws = [
+            shared.tile([P, 256], U8, name="ws0", align_bytes=64, offset=4096),
+            sb.tile([P, 256], U8, name="ws1", align_bytes=64),
+        ]
+        for u in range(2):
+            for e in range(2):
+                copy = nc.scalar.copy if (u, e) == (0, 0) else nc.vector.tensor_copy
+                interleave(copy, wb[2 * u + e][:], wa_raw[u][:, :, 128 * e : 128 * (e + 1)])
+            for e in range(2):
+                cols = slice(128 * e, 128 * (e + 1))
+                quantize(nc, wc[u][:, cols], ws[u][:, cols], wb[2 * u + e][:])
+
         w1d = shared.tile([P, 2 * N], U8, name="w1d", align_bytes=64, offset=1024)
         nc.vector.tensor_copy(
             out=w1d[:].rearrange("p (t s b) -> p t s b", t=PACK, b=2),
             in_=w1w[:].rearrange("p (s t b) -> p t s b", t=PACK, b=2),
         )
-
-        w1sd = shared.tile([P, N], U8, name="w1sd", align_bytes=64, offset=2048)
+        w1sd = shared.tile([P, N], U8, name="w1sd", align_bytes=64, offset=0)
         nc.vector.tensor_copy(
             out=w1sd[:].rearrange("p (t s) -> p t s", t=PACK), in_=w1s[:].rearrange("p (s t) -> p t s", t=PACK)
         )
 
-        def first_product(acc, t, codes, scales):
+        g = sb.tile([P, PACK, V], F32, name="g", align_bytes=64)
+        act = [sb.tile([P, H], F32, name="act%d" % t, align_bytes=64) for t in range(PACK)]
+
+        def first_layer(t, u):
+            y = psum.tile([P, 256], F32, name="y", tag="bank")
             nc.tensor.matmul_mx(
-                out=acc,
+                out=y[:],
                 lhsT=xg[:, P * t : P * (t + 1)].bitcast(FP8X4),
                 lhsT_scale=xsd[:, P * t : P * (t + 1)],
-                rhs=codes.bitcast(FP8X4),
-                rhs_scale=scales,
+                rhs=wc[u][:].bitcast(FP8X4),
+                rhs_scale=ws[u][:],
                 start=True,
                 stop=True,
             )
+            nc.scalar.activation(out=act[t][:, 256 * u : 256 * (u + 1)], in_=y[:], func=SILU)
 
-        g = sb.tile([P, PACK, V], F32, name="g", align_bytes=64)
-        for t in range(PACK):
-            act = sb.tile([P, H], F32, name="act%d" % t, align_bytes=64)
-            if t == 0:
-                ya = psum.tile([P, EARLY], F32, name="ya", tag="bank")
-                yb = psum.tile([P, H - EARLY], F32, name="yb", tag="bank")
-                first_product(ya[:, 0:256], t, wc[:, 0:256], ws[:, 0:256])
-                first_product(ya[:, 256:EARLY], t, wc[:, 256:EARLY], ws[:, 256:EARLY])
-                first_product(yb[:], t, wc2[:], ws2[:])
-                nc.scalar.activation(out=act[:, 0:EARLY], in_=ya[:], func=SILU)
-                nc.scalar.activation(out=act[:, EARLY:H], in_=yb[:], func=SILU)
-            else:
-                y = psum.tile([P, H], F32, name="y", tag="bank")
-                first_product(y[:, 0:256], t, wc[:, 0:256], ws[:, 0:256])
-                first_product(y[:, 256:EARLY], t, wc[:, 256:EARLY], ws[:, 256:EARLY])
-                first_product(y[:, EARLY:H], t, wc2[:], ws2[:])
-                nc.scalar.activation(out=act[:], in_=y[:], func=SILU)
-            if t < PACK - 1:
-                nc.vector.tensor_tensor(out=g[:, t, :], in0=act[:].indirect(fl_sb[:]), in1=gtb[:, t, :], op=MULT)
-            else:
-                for h in range(2):
-                    cols = slice(HALF * h, HALF * (h + 1))
-                    nc.vector.tensor_tensor(
-                        out=g[:, t, cols],
-                        in0=act[:].indirect(fl_sb[:, 8 * h : 8 * h + 8]),
-                        in1=gtb[:, t, cols],
-                        op=MULT,
-                    )
+        for t in range(PACK - 1):
+            first_layer(t, 0)
+        for t in range(PACK - 1):
+            first_layer(t, 1)
+            nc.vector.tensor_tensor(out=g[:, t, :], in0=act[t][:].indirect(fl_sb[:]), in1=gtb[:, t, :], op=MULT)
+        t = PACK - 1
+        first_layer(t, 0)
+        first_layer(t, 1)
+        for h in range(2):
+            cols = slice(HALF * h, HALF * (h + 1))
+            nc.vector.tensor_tensor(
+                out=g[:, t, cols], in0=act[t][:].indirect(fl_sb[:, 8 * h : 8 * h + 8]), in1=gtb[:, t, cols], op=MULT
+            )
 
         zb = [sb.tile([P, HALF, PACK], BF16, name="zb%d" % h, align_bytes=64) for h in range(2)]
         zc = [sb.tile([P, HALF], I32, name="zc%d" % h, align_bytes=64) for h in range(2)]
         zs = [sb.tile([P, HALF], U8, name="zs%d" % h, align_bytes=64) for h in range(2)]
         for h in range(2):
-            interleave(nc.vector.tensor_copy, zb[h][:], g[:, :, HALF * h : HALF * (h + 1)])
+            interleave(nc.scalar.copy if h == 0 else nc.vector.tensor_copy, zb[h][:], g[:, :, HALF * h : HALF * (h + 1)])
         for h in range(2):
             quantize(nc, zc[h][:], zs[h][:], zb[h][:])
 

@@ -37,7 +37,7 @@ def tile_picked_tokmixl_silu_po_kernel(
     with ExitStack() as ctx:
         sb = ctx.enter_context(tc.tile_pool(name="sb", bufs=1))
         shared = ctx.enter_context(tc.tile_pool(name="shared", bufs=1))
-        psum = ctx.enter_context(tc.psum_pool(name="psum", bufs=8))
+        psum = ctx.enter_context(tc.psum_pool(name="psum", bufs=1))
 
         offs_sb = sb.tile([P, S // 16], U16, name="offs_sb")
         fl_sb = sb.tile([P, V // 16], U16, name="fl_sb")
@@ -56,17 +56,17 @@ def tile_picked_tokmixl_silu_po_kernel(
         nc.vector.memset(warm_in[:], 0.0)
         nc.gpsimd.memset(w1s[:].bitcast(I32), 0)
 
+        nc.sync.dma_start(out=w1w[:].bitcast(I32), in_=w1_words[0].bitcast(I32))
         nc.sync.dma_start(offs_sb[:], offs)
         nc.sync.dma_start(out=gt_sb[:], in_=gt.rearrange("(p t) o -> p (t o)", t=PACK))
-        nc.sync.dma_start(fl_sb[:], fl)
         for q in range(4):
-            nc.sync.dma_start(
+            (nc.sync if q < 2 else nc.scalar).dma_start(
                 out=xs[32 * q : 32 * q + 4, :].bitcast(I32), in_=x_scales[0, 4 * q : 4 * q + 4, :].bitcast(I32)
             )
         nc.sync.dma_start(out=xw[:], in_=x_words[0].rearrange("p n t -> p (n t)").bitcast(I32))
         for u in range(2):
             nc.sync.dma_start(out=wa_raw[u][:], in_=wa_rows[:, :, 256 * u : 256 * (u + 1)])
-        nc.sync.dma_start(out=w1w[:].bitcast(I32), in_=w1_words[0].bitcast(I32))
+        nc.sync.dma_start(fl_sb[:], fl)
         for q in range(4):
             nc.sync.dma_start(
                 out=w1s[32 * q : 32 * q + 4, :].bitcast(I32), in_=w1_scales[0, 4 * q : 4 * q + 4, :].bitcast(I32)
@@ -76,6 +76,15 @@ def tile_picked_tokmixl_silu_po_kernel(
 
         gtb = sb.tile([P, PACK, V], F32, name="gtb", align_bytes=64)
         nc.scalar.copy(out=gtb[:], in_=gt_sb[:].unsqueeze(2).to_broadcast([P, PACK, V]))
+
+        w1d = sb.tile([P, 2 * N], U8, name="w1d", align_bytes=64)
+        nc.vector.tensor_copy(
+            out=w1d[:].rearrange("p (t s b) -> p t s b", t=PACK, b=2),
+            in_=w1w[:].rearrange("p (s t b) -> p t s b", t=PACK, b=2),
+        )
+
+        g = sb.tile([P, PACK, V], F32, name="g", align_bytes=64)
+        nc.scalar.copy(out=g[:, 2, HALF:V], in_=gt_sb[:, 3:4].to_broadcast([P, HALF]))
 
         xsg = sb.tile([P, S], U8, name="xsg", align_bytes=64)
         xsd = sb.tile([P, S], U8, name="xsd", align_bytes=64)
@@ -92,12 +101,12 @@ def tile_picked_tokmixl_silu_po_kernel(
         wb = [
             sb.tile([P, 128, PACK], BF16, name="wb0", align_bytes=64),
             shared.tile([P, 128, PACK], BF16, name="wb1", align_bytes=64, offset=2048),
-            shared.tile([P, 128, PACK], BF16, name="wb2", align_bytes=64, offset=0),
-            shared.tile([P, 128, PACK], BF16, name="wb3", align_bytes=64, offset=1024),
+            sb.tile([P, 128, PACK], BF16, name="wb2", align_bytes=64),
+            shared.tile([P, 128, PACK], BF16, name="wb3", align_bytes=64, offset=0),
         ]
         wc = [
             shared.tile([P, 256], I32, name="wc0", align_bytes=64, offset=3072),
-            sb.tile([P, 256], I32, name="wc1", align_bytes=64),
+            shared.tile([P, 256], I32, name="wc1", align_bytes=64, offset=5120),
         ]
         ws = [
             shared.tile([P, 256], U8, name="ws0", align_bytes=64, offset=4096),
@@ -105,27 +114,21 @@ def tile_picked_tokmixl_silu_po_kernel(
         ]
         for u in range(2):
             for e in range(2):
-                copy = nc.scalar.copy if (u, e) == (0, 0) else nc.vector.tensor_copy
+                copy = nc.scalar.copy if e == 0 else nc.vector.tensor_copy
                 interleave(copy, wb[2 * u + e][:], wa_raw[u][:, :, 128 * e : 128 * (e + 1)])
             for e in range(2):
                 cols = slice(128 * e, 128 * (e + 1))
                 quantize(nc, wc[u][:, cols], ws[u][:, cols], wb[2 * u + e][:])
 
-        w1d = shared.tile([P, 2 * N], U8, name="w1d", align_bytes=64, offset=1024)
-        nc.vector.tensor_copy(
-            out=w1d[:].rearrange("p (t s b) -> p t s b", t=PACK, b=2),
-            in_=w1w[:].rearrange("p (s t b) -> p t s b", t=PACK, b=2),
-        )
         w1sd = shared.tile([P, N], U8, name="w1sd", align_bytes=64, offset=0)
         nc.vector.tensor_copy(
             out=w1sd[:].rearrange("p (t s) -> p t s", t=PACK), in_=w1s[:].rearrange("p (s t) -> p t s", t=PACK)
         )
 
-        g = sb.tile([P, PACK, V], F32, name="g", align_bytes=64)
         act = [sb.tile([P, H], F32, name="act%d" % t, align_bytes=64) for t in range(PACK)]
 
-        def first_layer(t, u):
-            y = psum.tile([P, 256], F32, name="y", tag="bank")
+        def first_layer(t, u, bank):
+            y = psum.tile([P, 256], F32, name="y", tag="bank%d" % bank)
             nc.tensor.matmul_mx(
                 out=y[:],
                 lhsT=xg[:, P * t : P * (t + 1)].bitcast(FP8X4),
@@ -137,27 +140,32 @@ def tile_picked_tokmixl_silu_po_kernel(
             )
             nc.scalar.activation(out=act[t][:, 256 * u : 256 * (u + 1)], in_=y[:], func=SILU)
 
+        first_layer(0, 0, 0)
+        first_layer(1, 0, 1)
         for t in range(PACK - 1):
-            first_layer(t, 0)
-        for t in range(PACK - 1):
-            first_layer(t, 1)
-            nc.vector.tensor_tensor(out=g[:, t, :], in0=act[t][:].indirect(fl_sb[:]), in1=gtb[:, t, :], op=MULT)
+            first_layer(t, 1, 2 + t)
+            if t > 0:
+                first_layer(t + 1, 0, 1 + t)
+            if t < 2:
+                nc.vector.tensor_tensor(out=g[:, t, :], in0=act[t][:].indirect(fl_sb[:]), in1=gtb[:, t, :], op=MULT)
         t = PACK - 1
-        first_layer(t, 0)
-        first_layer(t, 1)
+        first_layer(t, 1, 2 + t)
         for h in range(2):
             cols = slice(HALF * h, HALF * (h + 1))
-            nc.vector.tensor_tensor(
-                out=g[:, t, cols], in0=act[t][:].indirect(fl_sb[:, 8 * h : 8 * h + 8]), in1=gtb[:, t, cols], op=MULT
-            )
+            for t in (2, 3):
+                gate = g[:, 2, HALF:V] if (t, h) == (3, 0) else gtb[:, t, cols]
+                nc.vector.tensor_tensor(
+                    out=g[:, t, cols], in0=act[t][:].indirect(fl_sb[:, 8 * h : 8 * h + 8]), in1=gate, op=MULT
+                )
 
         zb = [sb.tile([P, HALF, PACK], BF16, name="zb%d" % h, align_bytes=64) for h in range(2)]
         zc = [sb.tile([P, HALF], I32, name="zc%d" % h, align_bytes=64) for h in range(2)]
         zs = [sb.tile([P, HALF], U8, name="zs%d" % h, align_bytes=64) for h in range(2)]
-        for h in range(2):
-            interleave(nc.scalar.copy if h == 0 else nc.vector.tensor_copy, zb[h][:], g[:, :, HALF * h : HALF * (h + 1)])
-        for h in range(2):
-            quantize(nc, zc[h][:], zs[h][:], zb[h][:])
+        interleave(nc.scalar.copy, zb[0][:], g[:, :, 0:HALF])
+        quantize(nc, zc[0][:], zs[0][:], zb[0][:])
+        interleave(nc.vector.tensor_copy, zb[1][:, 0:80, :], g[:, :, HALF : HALF + 80])
+        interleave(nc.scalar.copy, zb[1][:, 80:HALF, :], g[:, :, HALF + 80 : V])
+        quantize(nc, zc[1][:], zs[1][:], zb[1][:])
 
         o32 = sb.tile([P, PACK, V], F32, name="o32", align_bytes=64)
         ob = [sb.tile([P, HALF, PACK], BF16, name="ob%d" % h, align_bytes=64) for h in range(2)]
@@ -168,7 +176,7 @@ def tile_picked_tokmixl_silu_po_kernel(
         for h in range(2):
             cols = slice(HALF * h, HALF * (h + 1))
             for u in range(2):
-                acc = psum.tile([P, 2, HALF], F32, name="acc", tag="bank")
+                acc = psum.tile([P, 2, HALF], F32, name="acc", tag="bank%d" % ((6 + 2 * h + u) % 8))
                 for e in range(2):
                     t = 2 * u + e
                     nc.tensor.matmul_mx(
@@ -183,7 +191,11 @@ def tile_picked_tokmixl_silu_po_kernel(
                 nc.scalar.copy(out=o32[:, 2 * u : 2 * u + 2, cols], in_=acc[:])
                 if h == 1:
                     nc.sync.dma_start(out=out_rows[:, 2 * u : 2 * u + 2, :], in_=o32[:, 2 * u : 2 * u + 2, :])
-            interleave(nc.vector.tensor_copy, ob[h][:], o32[:, :, cols])
+            if h == 0:
+                interleave(nc.vector.tensor_copy, ob[h][:], o32[:, :, cols])
+            else:
+                interleave(nc.vector.tensor_copy, ob[h][:, 0:96, :], o32[:, :, HALF : HALF + 96])
+                interleave(nc.scalar.copy, ob[h][:, 96:HALF, :], o32[:, :, HALF + 96 : V])
             quantize(nc, oc[:, cols], osc[:, cols], ob[h][:])
             nc.sync.dma_start(out=out_words[:, cols], in_=oc[:, cols])
         for q in range(4):

@@ -74,8 +74,10 @@ def tile_picked_tokmixl_silu_po_kernel(
 
         nc.scalar.activation(out=warm_out[:], in_=warm_in[:], func=SILU)
 
-        gtb = sb.tile([P, PACK, V], F32, name="gtb", align_bytes=64)
-        nc.scalar.copy(out=gtb[:], in_=gt_sb[:].unsqueeze(2).to_broadcast([P, PACK, V]))
+        gtb = sb.tile([P, 2, V], F32, name="gtb", align_bytes=64)
+        gth = sb.tile([P, 2, HALF], F32, name="gth", align_bytes=64)
+        nc.scalar.copy(out=gtb[:], in_=gt_sb[:, 0:2].unsqueeze(2).to_broadcast([P, 2, V]))
+        nc.scalar.copy(out=gth[:], in_=gt_sb[:, 2:4].unsqueeze(2).to_broadcast([P, 2, HALF]))
 
         w1d = sb.tile([P, 2 * N], U8, name="w1d", align_bytes=64)
         nc.vector.tensor_copy(
@@ -138,7 +140,7 @@ def tile_picked_tokmixl_silu_po_kernel(
                 start=True,
                 stop=True,
             )
-            nc.scalar.activation(out=act[t][:, 256 * u : 256 * (u + 1)], in_=y[:], func=SILU)
+            nc.scalar.activation(out=act[t][:, 256 * u : 256 * (u + 1)], in_=y[:], func=SILU, bias=warm_out[:])
 
         first_layer(0, 0, 0)
         first_layer(1, 0, 1)
@@ -153,7 +155,7 @@ def tile_picked_tokmixl_silu_po_kernel(
         for h in range(2):
             cols = slice(HALF * h, HALF * (h + 1))
             for t in (2, 3):
-                gate = g[:, 2, HALF:V] if (t, h) == (3, 0) else gtb[:, t, cols]
+                gate = g[:, 2, HALF:V] if (t, h) == (3, 0) else gth[:, t - 2, :]
                 nc.vector.tensor_tensor(
                     out=g[:, t, cols], in0=act[t][:].indirect(fl_sb[:, 8 * h : 8 * h + 8]), in1=gate, op=MULT
                 )
@@ -188,15 +190,22 @@ def tile_picked_tokmixl_silu_po_kernel(
                         start=True,
                         stop=True,
                     )
-                nc.scalar.copy(out=o32[:, 2 * u : 2 * u + 2, cols], in_=acc[:])
+                if (h, u) == (1, 1):
+                    for c in (0, 64):
+                        nc.scalar.copy(out=o32[:, 2:4, HALF + c : HALF + c + 64], in_=acc[:, :, c : c + 64])
+                else:
+                    nc.scalar.copy(out=o32[:, 2 * u : 2 * u + 2, cols], in_=acc[:])
                 if h == 1:
                     nc.sync.dma_start(out=out_rows[:, 2 * u : 2 * u + 2, :], in_=o32[:, 2 * u : 2 * u + 2, :])
             if h == 0:
                 interleave(nc.vector.tensor_copy, ob[h][:], o32[:, :, cols])
+                quantize(nc, oc[:, cols], osc[:, cols], ob[h][:])
             else:
-                interleave(nc.vector.tensor_copy, ob[h][:, 0:96, :], o32[:, :, HALF : HALF + 96])
-                interleave(nc.scalar.copy, ob[h][:, 96:HALF, :], o32[:, :, HALF + 96 : V])
-            quantize(nc, oc[:, cols], osc[:, cols], ob[h][:])
+                for c in (0, 64):
+                    interleave(nc.vector.tensor_copy, ob[h][:, c : c + 64, :], o32[:, :, HALF + c : HALF + c + 64])
+                for c in (0, 64):
+                    part = slice(HALF + c, HALF + c + 64)
+                    quantize(nc, oc[:, part], osc[:, part], ob[h][:, c : c + 64, :])
             nc.sync.dma_start(out=out_words[:, cols], in_=oc[:, cols])
         for q in range(4):
             eng = nc.scalar if q < 2 else nc.sync

@@ -18,7 +18,6 @@ MULT = mybir.AluOpType.mult
 
 P = 128
 PACK = 4
-EARLY = 384
 HALF = V // 2
 
 
@@ -61,7 +60,7 @@ def tile_picked_tokmixl_silu_po_kernel(
         nc.sync.dma_start(out=gt_sb[:], in_=gt.rearrange("(p t) o -> p (t o)", t=PACK))
         for q in range(4):
             (nc.sync if q < 2 else nc.scalar).dma_start(
-                out=xs[32 * q : 32 * q + 4, :].bitcast(I32), in_=x_scales[0, 4 * q : 4 * q + 4, :].bitcast(I32)
+                out=xs[q:P:32, :].bitcast(I32), in_=x_scales[0, q:16:4, :].bitcast(I32)
             )
         nc.sync.dma_start(out=xw[:], in_=x_words[0].rearrange("p n t -> p (n t)").bitcast(I32))
         for u in range(2):
@@ -69,7 +68,7 @@ def tile_picked_tokmixl_silu_po_kernel(
         nc.sync.dma_start(fl_sb[:], fl)
         for q in range(4):
             nc.sync.dma_start(
-                out=w1s[32 * q : 32 * q + 4, :].bitcast(I32), in_=w1_scales[0, 4 * q : 4 * q + 4, :].bitcast(I32)
+                out=w1s[q:P:32, :].bitcast(I32), in_=w1_scales[0, q:16:4, :].bitcast(I32)
             )
 
         nc.scalar.activation(out=warm_out[:], in_=warm_in[:], func=SILU)
@@ -196,8 +195,9 @@ def tile_picked_tokmixl_silu_po_kernel(
                 else:
                     nc.scalar.copy(out=o32[:, 2 * u : 2 * u + 2, cols], in_=acc[:])
                 if h == 1:
-                    nc.sync.dma_start(out=out_rows[:, 2 * u : 2 * u + 2, :], in_=o32[:, 2 * u : 2 * u + 2, :])
+                    nc.sync.dma_start(out=out_rows[:, 2 * u : 2 * u + 2, cols], in_=o32[:, 2 * u : 2 * u + 2, cols])
             if h == 0:
+                nc.sync.dma_start(out=out_rows[:, :, cols], in_=o32[:, :, cols])
                 interleave(nc.vector.tensor_copy, ob[h][:], o32[:, :, cols])
                 quantize(nc, oc[:, cols], osc[:, cols], ob[h][:])
             else:
@@ -210,5 +210,5 @@ def tile_picked_tokmixl_silu_po_kernel(
         for q in range(4):
             eng = nc.scalar if q < 2 else nc.sync
             eng.dma_start(
-                out=out_2[0, 4 * q : 4 * q + 4, :].bitcast(I32), in_=osc[32 * q : 32 * q + 4, :].bitcast(I32)
+                out=out_2[0, q:16:4, :].bitcast(I32), in_=osc[q:P:32, :].bitcast(I32)
             )

@@ -19,6 +19,7 @@ MULT = mybir.AluOpType.mult
 P = 128
 PACK = 4
 HALF = V // 2
+X_FIRST = 512
 
 
 def interleave(copy, dst, src):
@@ -55,17 +56,19 @@ def tile_picked_tokmixl_silu_po_kernel(
         nc.vector.memset(warm_in[:], 0.0)
         nc.gpsimd.memset(w1s[:].bitcast(I32), 0)
 
-        nc.sync.dma_start(out=w1w[:].bitcast(I32), in_=w1_words[0].bitcast(I32))
+        x_rows = x_words[0].rearrange("p n t -> p (n t)").bitcast(I32)
         nc.sync.dma_start(offs_sb[:], offs)
         nc.sync.dma_start(out=gt_sb[:], in_=gt.rearrange("(p t) o -> p (t o)", t=PACK))
+        nc.sync.dma_start(out=xw[:, 0:X_FIRST], in_=x_rows[:, 0:X_FIRST])
         for q in range(4):
-            (nc.sync if q < 2 else nc.scalar).dma_start(
+            nc.sync.dma_start(
                 out=xs[q:P:32, :].bitcast(I32), in_=x_scales[0, q:16:4, :].bitcast(I32)
             )
-        nc.sync.dma_start(out=xw[:], in_=x_words[0].rearrange("p n t -> p (n t)").bitcast(I32))
+        nc.sync.dma_start(out=xw[:, X_FIRST:T], in_=x_rows[:, X_FIRST:T])
         for u in range(2):
             nc.sync.dma_start(out=wa_raw[u][:], in_=wa_rows[:, :, 256 * u : 256 * (u + 1)])
         nc.sync.dma_start(fl_sb[:], fl)
+        nc.sync.dma_start(out=w1w[:].bitcast(I32), in_=w1_words[0].bitcast(I32))
         for q in range(4):
             nc.sync.dma_start(
                 out=w1s[q:P:32, :].bitcast(I32), in_=w1_scales[0, q:16:4, :].bitcast(I32)
@@ -77,12 +80,6 @@ def tile_picked_tokmixl_silu_po_kernel(
         gth = sb.tile([P, 2, HALF], F32, name="gth", align_bytes=64)
         nc.scalar.copy(out=gtb[:], in_=gt_sb[:, 0:2].unsqueeze(2).to_broadcast([P, 2, V]))
         nc.scalar.copy(out=gth[:], in_=gt_sb[:, 2:4].unsqueeze(2).to_broadcast([P, 2, HALF]))
-
-        w1d = sb.tile([P, 2 * N], U8, name="w1d", align_bytes=64)
-        nc.vector.tensor_copy(
-            out=w1d[:].rearrange("p (t s b) -> p t s b", t=PACK, b=2),
-            in_=w1w[:].rearrange("p (s t b) -> p t s b", t=PACK, b=2),
-        )
 
         g = sb.tile([P, PACK, V], F32, name="g", align_bytes=64)
         nc.scalar.copy(out=g[:, 2, HALF:V], in_=gt_sb[:, 3:4].to_broadcast([P, HALF]))
@@ -103,7 +100,7 @@ def tile_picked_tokmixl_silu_po_kernel(
             sb.tile([P, 128, PACK], BF16, name="wb0", align_bytes=64),
             shared.tile([P, 128, PACK], BF16, name="wb1", align_bytes=64, offset=2048),
             sb.tile([P, 128, PACK], BF16, name="wb2", align_bytes=64),
-            shared.tile([P, 128, PACK], BF16, name="wb3", align_bytes=64, offset=0),
+            shared.tile([P, 128, PACK], BF16, name="wb3", align_bytes=64, offset=1024),
         ]
         wc = [
             shared.tile([P, 256], I32, name="wc0", align_bytes=64, offset=3072),
@@ -121,7 +118,12 @@ def tile_picked_tokmixl_silu_po_kernel(
                 cols = slice(128 * e, 128 * (e + 1))
                 quantize(nc, wc[u][:, cols], ws[u][:, cols], wb[2 * u + e][:])
 
-        w1sd = shared.tile([P, N], U8, name="w1sd", align_bytes=64, offset=0)
+        w1d = shared.tile([P, 2 * N], U8, name="w1d", align_bytes=64, offset=64)
+        w1sd = shared.tile([P, N], U8, name="w1sd", align_bytes=64, offset=1024 + 64)
+        nc.vector.tensor_copy(
+            out=w1d[:].bitcast(U16).rearrange("p (t s) -> p t s", t=PACK),
+            in_=w1w[:].bitcast(U16).rearrange("p (s t) -> p t s", t=PACK),
+        )
         nc.vector.tensor_copy(
             out=w1sd[:].rearrange("p (t s) -> p t s", t=PACK), in_=w1s[:].rearrange("p (s t) -> p t s", t=PACK)
         )
@@ -194,10 +196,8 @@ def tile_picked_tokmixl_silu_po_kernel(
                         nc.scalar.copy(out=o32[:, 2:4, HALF + c : HALF + c + 64], in_=acc[:, :, c : c + 64])
                 else:
                     nc.scalar.copy(out=o32[:, 2 * u : 2 * u + 2, cols], in_=acc[:])
-                if h == 1:
-                    nc.sync.dma_start(out=out_rows[:, 2 * u : 2 * u + 2, cols], in_=o32[:, 2 * u : 2 * u + 2, cols])
+            nc.sync.dma_start(out=out_rows[:, :, cols], in_=o32[:, :, cols])
             if h == 0:
-                nc.sync.dma_start(out=out_rows[:, :, cols], in_=o32[:, :, cols])
                 interleave(nc.vector.tensor_copy, ob[h][:], o32[:, :, cols])
                 quantize(nc, oc[:, cols], osc[:, cols], ob[h][:])
             else:

@@ -14,6 +14,7 @@ U8 = mybir.dt.uint8
 FP8X4 = mybir.dt.float8_e4m3fn_x4
 FP4X4 = mybir.dt.float4_e2m1fn_x4
 SILU = mybir.ActivationFunctionType.Silu
+COPY = mybir.ActivationFunctionType.Copy
 MULT = mybir.AluOpType.mult
 
 P = 128
@@ -43,7 +44,10 @@ def tile_picked_tokmixl_silu_po_kernel(
         fl_sb = sb.tile([P, V // 16], U16, name="fl_sb")
         xw = shared.tile([P, T], I32, name="xw", align_bytes=64, offset=0)
         xs = sb.tile([P, T], U8, name="xs", align_bytes=64)
-        wa_raw = [sb.tile([P, PACK, 256], F32, name="wa_raw%d" % u, align_bytes=64) for u in range(2)]
+        wa_raw = [
+            sb.tile([P, PACK, 256], F32, name="wa_raw0", align_bytes=64),
+            shared.tile([P, PACK, 256], F32, name="wa_raw1", align_bytes=64, offset=8192 + 1024),
+        ]
         w1w = sb.tile([P, 2 * N], U8, name="w1w", align_bytes=64)
         w1s = sb.tile([P, N], U8, name="w1s", align_bytes=64)
         gt_sb = sb.tile([P, PACK], F32, name="gt_sb", align_bytes=64)
@@ -76,9 +80,7 @@ def tile_picked_tokmixl_silu_po_kernel(
 
         nc.scalar.activation(out=warm_out[:], in_=warm_in[:], func=SILU)
 
-        gtb = sb.tile([P, 2, V], F32, name="gtb", align_bytes=64)
         gth = sb.tile([P, 2, HALF], F32, name="gth", align_bytes=64)
-        nc.scalar.copy(out=gtb[:], in_=gt_sb[:, 0:2].unsqueeze(2).to_broadcast([P, 2, V]))
         nc.scalar.copy(out=gth[:], in_=gt_sb[:, 2:4].unsqueeze(2).to_broadcast([P, 2, HALF]))
 
         g = sb.tile([P, PACK, V], F32, name="g", align_bytes=64)
@@ -128,12 +130,11 @@ def tile_picked_tokmixl_silu_po_kernel(
             out=w1sd[:].rearrange("p (t s) -> p t s", t=PACK), in_=w1s[:].rearrange("p (s t) -> p t s", t=PACK)
         )
 
-        act = [sb.tile([P, H], F32, name="act%d" % t, align_bytes=64) for t in range(PACK)]
+        act = [shared.tile([P, H], F32, name="act%d" % t, align_bytes=64, offset=8192 + 2048 * t) for t in range(PACK)]
 
-        def first_layer(t, u, bank):
-            y = psum.tile([P, 256], F32, name="y", tag="bank%d" % bank)
+        def project(out, t, u):
             nc.tensor.matmul_mx(
-                out=y[:],
+                out=out,
                 lhsT=xg[:, P * t : P * (t + 1)].bitcast(FP8X4),
                 lhsT_scale=xsd[:, P * t : P * (t + 1)],
                 rhs=wc[u][:].bitcast(FP8X4),
@@ -141,18 +142,25 @@ def tile_picked_tokmixl_silu_po_kernel(
                 start=True,
                 stop=True,
             )
+
+        def first_layer(t, u, bank):
+            y = psum.tile([P, 256], F32, name="y", tag="bank%d" % bank)
+            project(y[:], t, u)
             nc.scalar.activation(out=act[t][:, 256 * u : 256 * (u + 1)], in_=y[:], func=SILU, bias=warm_out[:])
 
-        first_layer(0, 0, 0)
-        first_layer(1, 0, 1)
-        for t in range(PACK - 1):
-            first_layer(t, 1, 2 + t)
-            if t > 0:
-                first_layer(t + 1, 0, 1 + t)
-            if t < 2:
-                nc.vector.tensor_tensor(out=g[:, t, :], in0=act[t][:].indirect(fl_sb[:]), in1=gtb[:, t, :], op=MULT)
-        t = PACK - 1
-        first_layer(t, 1, 2 + t)
+        for u in range(2):
+            for t in range(PACK - 1):
+                first_layer(t, u, 3 * u + t)
+        last = psum.tile([P, H], F32, name="last", tag="bank0")
+        for u in range(2):
+            project(last[:, 256 * u : 256 * (u + 1)], 3, u)
+        nc.scalar.activation(out=act[3][:], in_=last[:], func=SILU, bias=warm_out[:])
+
+        picked = sb.tile([P, 2, V], F32, name="picked", align_bytes=64)
+        for t in range(2):
+            nc.vector.tensor_copy(out=picked[:, t, :], in_=act[t][:].indirect(fl_sb[:]))
+        for t in range(2):
+            nc.scalar.activation(out=g[:, t, :], in_=picked[:, t, :], func=COPY, scale=gt_sb[:, t : t + 1])
         for h in range(2):
             cols = slice(HALF * h, HALF * (h + 1))
             for t in (2, 3):
@@ -179,7 +187,7 @@ def tile_picked_tokmixl_silu_po_kernel(
         for h in range(2):
             cols = slice(HALF * h, HALF * (h + 1))
             for u in range(2):
-                acc = psum.tile([P, 2, HALF], F32, name="acc", tag="bank%d" % ((6 + 2 * h + u) % 8))
+                acc = psum.tile([P, 2, HALF], F32, name="acc", tag="bank%d" % ((6 + 3 * h + u) % 8))
                 for e in range(2):
                     t = 2 * u + e
                     nc.tensor.matmul_mx(

@@ -14,7 +14,6 @@ U8 = mybir.dt.uint8
 FP8X4 = mybir.dt.float8_e4m3fn_x4
 FP4X4 = mybir.dt.float4_e2m1fn_x4
 SILU = mybir.ActivationFunctionType.Silu
-COPY = mybir.ActivationFunctionType.Copy
 MULT = mybir.AluOpType.mult
 
 P = 128
@@ -58,12 +57,12 @@ def tile_picked_tokmixl_silu_po_kernel(
 
         nc.vector.memset(xs[:].bitcast(I32), 0)
         nc.vector.memset(warm_in[:], 0.0)
-        nc.gpsimd.memset(w1s[:].bitcast(I32), 0)
+        nc.vector.memset(w1s[:].bitcast(I32), 0)
 
         x_rows = x_words[0].rearrange("p n t -> p (n t)").bitcast(I32)
         nc.sync.dma_start(offs_sb[:], offs)
-        nc.sync.dma_start(out=gt_sb[:], in_=gt.rearrange("(p t) o -> p (t o)", t=PACK))
         nc.sync.dma_start(out=xw[:, 0:X_FIRST], in_=x_rows[:, 0:X_FIRST])
+        nc.sync.dma_start(out=gt_sb[:], in_=gt.rearrange("(p t) o -> p (t o)", t=PACK))
         for q in range(4):
             nc.sync.dma_start(
                 out=xs[q:P:32, :].bitcast(I32), in_=x_scales[0, q:16:4, :].bitcast(I32)
@@ -71,16 +70,18 @@ def tile_picked_tokmixl_silu_po_kernel(
         nc.sync.dma_start(out=xw[:, X_FIRST:T], in_=x_rows[:, X_FIRST:T])
         for u in range(2):
             nc.sync.dma_start(out=wa_raw[u][:], in_=wa_rows[:, :, 256 * u : 256 * (u + 1)])
-        nc.sync.dma_start(fl_sb[:], fl)
         nc.sync.dma_start(out=w1w[:].bitcast(I32), in_=w1_words[0].bitcast(I32))
         for q in range(4):
             nc.sync.dma_start(
                 out=w1s[q:P:32, :].bitcast(I32), in_=w1_scales[0, q:16:4, :].bitcast(I32)
             )
+        nc.sync.dma_start(fl_sb[:], fl)
 
         nc.scalar.activation(out=warm_out[:], in_=warm_in[:], func=SILU)
 
+        gtb = sb.tile([P, 2, V], F32, name="gtb", align_bytes=64)
         gth = sb.tile([P, 2, HALF], F32, name="gth", align_bytes=64)
+        nc.scalar.copy(out=gtb[:], in_=gt_sb[:, 0:2].unsqueeze(2).to_broadcast([P, 2, V]))
         nc.scalar.copy(out=gth[:], in_=gt_sb[:, 2:4].unsqueeze(2).to_broadcast([P, 2, HALF]))
 
         g = sb.tile([P, PACK, V], F32, name="g", align_bytes=64)
@@ -104,21 +105,15 @@ def tile_picked_tokmixl_silu_po_kernel(
             sb.tile([P, 128, PACK], BF16, name="wb2", align_bytes=64),
             shared.tile([P, 128, PACK], BF16, name="wb3", align_bytes=64, offset=1024),
         ]
-        wc = [
-            shared.tile([P, 256], I32, name="wc0", align_bytes=64, offset=3072),
-            shared.tile([P, 256], I32, name="wc1", align_bytes=64, offset=5120),
-        ]
-        ws = [
-            shared.tile([P, 256], U8, name="ws0", align_bytes=64, offset=4096),
-            sb.tile([P, 256], U8, name="ws1", align_bytes=64),
-        ]
+        wc = shared.tile([P, H], I32, name="wc", align_bytes=64, offset=3072)
+        ws = shared.tile([P, H], U8, name="ws", align_bytes=64, offset=5120)
         for u in range(2):
             for e in range(2):
                 copy = nc.scalar.copy if e == 0 else nc.vector.tensor_copy
                 interleave(copy, wb[2 * u + e][:], wa_raw[u][:, :, 128 * e : 128 * (e + 1)])
-            for e in range(2):
-                cols = slice(128 * e, 128 * (e + 1))
-                quantize(nc, wc[u][:, cols], ws[u][:, cols], wb[2 * u + e][:])
+            for e in (1, 0):
+                cols = slice(256 * u + 128 * e, 256 * u + 128 * (e + 1))
+                quantize(nc, wc[:, cols], ws[:, cols], wb[2 * u + e][:])
 
         w1d = shared.tile([P, 2 * N], U8, name="w1d", align_bytes=64, offset=64)
         w1sd = shared.tile([P, N], U8, name="w1sd", align_bytes=64, offset=1024 + 64)
@@ -132,35 +127,40 @@ def tile_picked_tokmixl_silu_po_kernel(
 
         act = [shared.tile([P, H], F32, name="act%d" % t, align_bytes=64, offset=8192 + 2048 * t) for t in range(PACK)]
 
-        def project(out, t, u):
+        def project(out, t, cols):
             nc.tensor.matmul_mx(
                 out=out,
                 lhsT=xg[:, P * t : P * (t + 1)].bitcast(FP8X4),
                 lhsT_scale=xsd[:, P * t : P * (t + 1)],
-                rhs=wc[u][:].bitcast(FP8X4),
-                rhs_scale=ws[u][:],
+                rhs=wc[:, cols].bitcast(FP8X4),
+                rhs_scale=ws[:, cols],
                 start=True,
                 stop=True,
             )
 
-        def first_layer(t, u, bank):
-            y = psum.tile([P, 256], F32, name="y", tag="bank%d" % bank)
-            project(y[:], t, u)
-            nc.scalar.activation(out=act[t][:, 256 * u : 256 * (u + 1)], in_=y[:], func=SILU, bias=warm_out[:])
+        def activate(t, cols, y):
+            nc.scalar.activation(out=act[t][:, cols], in_=y, func=SILU)
 
-        for u in range(2):
-            for t in range(PACK - 1):
-                first_layer(t, u, 3 * u + t)
-        last = psum.tile([P, H], F32, name="last", tag="bank0")
-        for u in range(2):
-            project(last[:, 256 * u : 256 * (u + 1)], 3, u)
-        nc.scalar.activation(out=act[3][:], in_=last[:], func=SILU, bias=warm_out[:])
+        early = [psum.tile([P, 256], F32, name="early%d" % t, tag="bank%d" % t) for t in range(2)]
+        for cols in (slice(128, 256), slice(0, 128)):
+            for t in range(2):
+                project(early[t][:, cols], t, cols)
+        for t in range(2):
+            activate(t, slice(0, 256), early[t][:])
+        whole = psum.tile([P, H], F32, name="whole", tag="bank4")
+        project(whole[:, 0:256], 2, slice(0, 256))
+        for t, cols, bank in ((0, slice(384, 512), 5), (0, slice(256, 384), 2), (1, slice(256, 512), 3)):
+            y = psum.tile([P, cols.stop - cols.start], F32, name="y", tag="bank%d" % bank)
+            project(y[:], t, cols)
+            activate(t, cols, y[:])
+        project(whole[:, 256:512], 2, slice(256, 512))
+        activate(2, slice(0, 512), whole[:])
+        last = psum.tile([P, H], F32, name="last", tag="bank1")
+        project(last[:], 3, slice(0, 512))
+        activate(3, slice(0, 512), last[:])
 
-        picked = sb.tile([P, 2, V], F32, name="picked", align_bytes=64)
         for t in range(2):
-            nc.vector.tensor_copy(out=picked[:, t, :], in_=act[t][:].indirect(fl_sb[:]))
-        for t in range(2):
-            nc.scalar.activation(out=g[:, t, :], in_=picked[:, t, :], func=COPY, scale=gt_sb[:, t : t + 1])
+            nc.vector.tensor_tensor(out=g[:, t, :], in0=act[t][:].indirect(fl_sb[:]), in1=gtb[:, t, :], op=MULT)
         for h in range(2):
             cols = slice(HALF * h, HALF * (h + 1))
             for t in (2, 3):
@@ -187,7 +187,7 @@ def tile_picked_tokmixl_silu_po_kernel(
         for h in range(2):
             cols = slice(HALF * h, HALF * (h + 1))
             for u in range(2):
-                acc = psum.tile([P, 2, HALF], F32, name="acc", tag="bank%d" % ((6 + 3 * h + u) % 8))
+                acc = psum.tile([P, 2, HALF], F32, name="acc", tag="bank%d" % ((5 + 2 * h + u) % 8))
                 for e in range(2):
                     t = 2 * u + e
                     nc.tensor.matmul_mx(

@@ -101,16 +101,18 @@ def tile_picked_tokmixl_silu_po_kernel(
 
         wb = [
             sb.tile([P, 128, PACK], BF16, name="wb0", align_bytes=64),
-            shared.tile([P, 128, PACK], BF16, name="wb1", align_bytes=64, offset=2048),
+            sb.tile([P, 128, PACK], BF16, name="wb1", align_bytes=64),
             sb.tile([P, 128, PACK], BF16, name="wb2", align_bytes=64),
             shared.tile([P, 128, PACK], BF16, name="wb3", align_bytes=64, offset=1024),
         ]
         wc = shared.tile([P, H], I32, name="wc", align_bytes=64, offset=3072)
         ws = shared.tile([P, H], U8, name="ws", align_bytes=64, offset=5120)
         for u in range(2):
-            for e in range(2):
-                copy = nc.scalar.copy if e == 0 else nc.vector.tensor_copy
-                interleave(copy, wb[2 * u + e][:], wa_raw[u][:, :, 128 * e : 128 * (e + 1)])
+            share = (128, 96)[u]
+            interleave(nc.scalar.copy, wb[2 * u][:, 0:share, :], wa_raw[u][:, :, 0:share])
+            interleave(nc.vector.tensor_copy, wb[2 * u + 1][:], wa_raw[u][:, :, 128:256])
+            if share < 128:
+                interleave(nc.vector.tensor_copy, wb[2 * u][:, share:128, :], wa_raw[u][:, :, share:128])
             for e in (1, 0):
                 cols = slice(256 * u + 128 * e, 256 * u + 128 * (e + 1))
                 quantize(nc, wc[:, cols], ws[:, cols], wb[2 * u + e][:])

@@ -20,6 +20,7 @@ P = 128
 PACK = 4
 HALF = V // 2
 X_FIRST = 512
+Z_VECTOR = (64, 72)
 
 
 def interleave(copy, dst, src):
@@ -79,13 +80,12 @@ def tile_picked_tokmixl_silu_po_kernel(
 
         nc.scalar.activation(out=warm_out[:], in_=warm_in[:], func=SILU)
 
-        gtb = sb.tile([P, 2, V], F32, name="gtb", align_bytes=64)
-        gth = sb.tile([P, 2, HALF], F32, name="gth", align_bytes=64)
-        nc.scalar.copy(out=gtb[:], in_=gt_sb[:, 0:2].unsqueeze(2).to_broadcast([P, 2, V]))
-        nc.scalar.copy(out=gth[:], in_=gt_sb[:, 2:4].unsqueeze(2).to_broadcast([P, 2, HALF]))
+        gtb = sb.tile([P, 3, V], F32, name="gtb", align_bytes=64)
+        gth = sb.tile([P, HALF], F32, name="gth", align_bytes=64)
+        nc.scalar.copy(out=gtb[:], in_=gt_sb[:, 0:3].unsqueeze(2).to_broadcast([P, 3, V]))
+        nc.scalar.copy(out=gth[:], in_=gt_sb[:, 3:4].to_broadcast([P, HALF]))
 
         g = sb.tile([P, PACK, V], F32, name="g", align_bytes=64)
-        nc.scalar.copy(out=g[:, 2, HALF:V], in_=gt_sb[:, 3:4].to_broadcast([P, HALF]))
 
         xsg = sb.tile([P, S], U8, name="xsg", align_bytes=64)
         xsd = sb.tile([P, S], U8, name="xsd", align_bytes=64)
@@ -161,24 +161,25 @@ def tile_picked_tokmixl_silu_po_kernel(
         project(last[:], 3, slice(0, 512))
         activate(3, slice(0, 512), last[:])
 
-        for t in range(2):
+        for t in range(3):
             nc.vector.tensor_tensor(out=g[:, t, :], in0=act[t][:].indirect(fl_sb[:]), in1=gtb[:, t, :], op=MULT)
         for h in range(2):
-            cols = slice(HALF * h, HALF * (h + 1))
-            for t in (2, 3):
-                gate = g[:, 2, HALF:V] if (t, h) == (3, 0) else gth[:, t - 2, :]
-                nc.vector.tensor_tensor(
-                    out=g[:, t, cols], in0=act[t][:].indirect(fl_sb[:, 8 * h : 8 * h + 8]), in1=gate, op=MULT
-                )
+            nc.vector.tensor_tensor(
+                out=g[:, 3, HALF * h : HALF * (h + 1)],
+                in0=act[3][:].indirect(fl_sb[:, 8 * h : 8 * h + 8]),
+                in1=gth[:],
+                op=MULT,
+            )
 
         zb = [sb.tile([P, HALF, PACK], BF16, name="zb%d" % h, align_bytes=64) for h in range(2)]
         zc = [sb.tile([P, HALF], I32, name="zc%d" % h, align_bytes=64) for h in range(2)]
         zs = [sb.tile([P, HALF], U8, name="zs%d" % h, align_bytes=64) for h in range(2)]
-        interleave(nc.scalar.copy, zb[0][:], g[:, :, 0:HALF])
-        quantize(nc, zc[0][:], zs[0][:], zb[0][:])
-        interleave(nc.vector.tensor_copy, zb[1][:, 0:80, :], g[:, :, HALF : HALF + 80])
-        interleave(nc.scalar.copy, zb[1][:, 80:HALF, :], g[:, :, HALF + 80 : V])
-        quantize(nc, zc[1][:], zs[1][:], zb[1][:])
+        for h in range(2):
+            split = HALF * h + Z_VECTOR[h]
+            interleave(nc.vector.tensor_copy, zb[h][:, 0 : Z_VECTOR[h], :], g[:, :, HALF * h : split])
+            interleave(nc.scalar.copy, zb[h][:, Z_VECTOR[h] : HALF, :], g[:, :, split : HALF * (h + 1)])
+        for h in range(2):
+            quantize(nc, zc[h][:], zs[h][:], zb[h][:])
 
         o32 = sb.tile([P, PACK, V], F32, name="o32", align_bytes=64)
         ob = [sb.tile([P, HALF, PACK], BF16, name="ob%d" % h, align_bytes=64) for h in range(2)]

@@ -189,10 +189,10 @@ def tile_picked_tokmixl_silu_po_kernel(
         out_words = out_1[0].rearrange("p n t -> p (n t)").bitcast(I32)
         for h in range(2):
             cols = slice(HALF * h, HALF * (h + 1))
-            for u in range(2):
-                acc = psum.tile([P, 2, HALF], F32, name="acc", tag="bank%d" % ((5 + 2 * h + u) % 8))
-                for e in range(2):
-                    t = 2 * u + e
+            groups = ((0, 1), (2, 3)) if h == 0 else ((0, 1), (2,), (3,))
+            for slots in groups:
+                acc = psum.tile([P, len(slots), HALF], F32, name="acc", tag="bank%d" % ((5 + 3 * h + slots[0]) % 8))
+                for e, t in enumerate(slots):
                     nc.tensor.matmul_mx(
                         out=acc[:, e, :],
                         lhsT=w1d[:, 2 * P * t : 2 * P * (t + 1)].bitcast(FP4X4),
@@ -202,18 +202,18 @@ def tile_picked_tokmixl_silu_po_kernel(
                         start=True,
                         stop=True,
                     )
-                if (h, u) == (1, 1):
+                if slots == (3,):
                     for c in (0, 64):
-                        nc.scalar.copy(out=o32[:, 2:4, HALF + c : HALF + c + 64], in_=acc[:, :, c : c + 64])
+                        nc.scalar.copy(out=o32[:, 3, HALF + c : HALF + c + 64], in_=acc[:, 0, c : c + 64])
                 else:
-                    nc.scalar.copy(out=o32[:, 2 * u : 2 * u + 2, cols], in_=acc[:])
+                    nc.scalar.copy(out=o32[:, slots[0] : slots[-1] + 1, cols], in_=acc[:])
             nc.sync.dma_start(out=out_rows[:, :, cols], in_=o32[:, :, cols])
             if h == 0:
                 interleave(nc.vector.tensor_copy, ob[h][:], o32[:, :, cols])
                 quantize(nc, oc[:, cols], osc[:, cols], ob[h][:])
             else:
-                for c in (0, 64):
-                    interleave(nc.vector.tensor_copy, ob[h][:, c : c + 64, :], o32[:, :, HALF + c : HALF + c + 64])
+                for c, copy in ((0, nc.vector.tensor_copy), (64, nc.scalar.copy)):
+                    interleave(copy, ob[h][:, c : c + 64, :], o32[:, :, HALF + c : HALF + c + 64])
                 for c in (0, 64):
                     part = slice(HALF + c, HALF + c + 64)
                     quantize(nc, oc[:, part], osc[:, part], ob[h][:, c : c + 64, :])

@@ -61,8 +61,8 @@ def tile_picked_tokmixl_silu_po_kernel(
         nc.vector.memset(w1s[:].bitcast(I32), 0)
 
         x_rows = x_words[0].rearrange("p n t -> p (n t)").bitcast(I32)
-        nc.sync.dma_start(offs_sb[:], offs)
         nc.sync.dma_start(out=xw[:, 0:X_FIRST], in_=x_rows[:, 0:X_FIRST])
+        nc.sync.dma_start(offs_sb[:], offs)
         nc.sync.dma_start(out=gt_sb[:], in_=gt.rearrange("(p t) o -> p (t o)", t=PACK))
         for q in range(4):
             nc.sync.dma_start(
@@ -117,12 +117,7 @@ def tile_picked_tokmixl_silu_po_kernel(
                 cols = slice(256 * u + 128 * e, 256 * u + 128 * (e + 1))
                 quantize(nc, wc[:, cols], ws[:, cols], wb[2 * u + e][:])
 
-        w1d = shared.tile([P, 2 * N], U8, name="w1d", align_bytes=64, offset=64)
         w1sd = shared.tile([P, N], U8, name="w1sd", align_bytes=64, offset=1024 + 64)
-        nc.vector.tensor_copy(
-            out=w1d[:].bitcast(U16).rearrange("p (t s) -> p t s", t=PACK),
-            in_=w1w[:].bitcast(U16).rearrange("p (s t) -> p t s", t=PACK),
-        )
         nc.vector.tensor_copy(
             out=w1sd[:].rearrange("p (t s) -> p t s", t=PACK), in_=w1s[:].rearrange("p (s t) -> p t s", t=PACK)
         )
@@ -160,6 +155,12 @@ def tile_picked_tokmixl_silu_po_kernel(
         last = psum.tile([P, H], F32, name="last", tag="bank1")
         project(last[:], 3, slice(0, 512))
         activate(3, slice(0, 512), last[:])
+
+        w1d = shared.tile([P, 2 * N], U8, name="w1d", align_bytes=64, offset=3072)
+        nc.scalar.copy(
+            out=w1d[:].bitcast(U16).rearrange("p (t s) -> p t s", t=PACK),
+            in_=w1w[:].bitcast(U16).rearrange("p (s t) -> p t s", t=PACK),
+        )
 
         for t in range(3):
             nc.vector.tensor_tensor(out=g[:, t, :], in0=act[t][:].indirect(fl_sb[:]), in1=gtb[:, t, :], op=MULT)

@@ -87,12 +87,15 @@ def tile_picked_tokmixl_silu_po_kernel(
 
         g = sb.tile([P, PACK, V], F32, name="g", align_bytes=64)
 
-        xsg = sb.tile([P, S], U8, name="xsg", align_bytes=64)
+        xsg = [sb.tile([P, S // 2], U8, name="xsg%d" % a, align_bytes=64) for a in range(2)]
         xsd = sb.tile([P, S], U8, name="xsd", align_bytes=64)
-        nc.vector.tensor_copy(out=xsg[:], in_=xs[:].indirect(offs_sb[:]))
-        nc.vector.tensor_copy(
-            out=xsd[:].rearrange("p (t s) -> p t s", t=PACK), in_=xsg[:].rearrange("p (s t) -> p t s", t=PACK)
-        )
+        for a in range(2):
+            nc.vector.tensor_copy(out=xsg[a][:], in_=xs[:].indirect(offs_sb[:, 16 * a : 16 * (a + 1)]))
+        for a in range(2):
+            nc.vector.tensor_copy(
+                out=xsd[:].rearrange("p (t s) -> p t s", t=PACK)[:, :, 64 * a : 64 * (a + 1)],
+                in_=xsg[a][:].rearrange("p (s t) -> p t s", t=PACK),
+            )
         xg = sb.tile([P, S], I32, name="xg", align_bytes=64)
         nc.vector.tensor_copy(
             out=xg[:].bitcast(U32).rearrange("p (t s) -> p s t", t=PACK),

@@ -24,7 +24,7 @@ Z_VECTOR = (64, 72)
 
 
 def interleave(copy, dst, src):
-    copy(out=dst.rearrange("p (c i) t -> p c t i", i=4), in_=src.rearrange("p t (c i) -> p c t i", i=4))
+    copy(out=dst.rearrange("p (c i) t -> p c t i", i=2), in_=src.rearrange("p t (c i) -> p c t i", i=2))
 
 
 def quantize(nc, codes, scales, grouped):

from contextlib import ExitStack

import concourse.mybir as mybir

K, T, S, V, N, H = 512, 2048, 512, 256, 512, 512
FLOPS = 2 * K * S * H + 2 * S * N * V

F32 = mybir.dt.float32
BF16 = mybir.dt.bfloat16
I32 = mybir.dt.int32
U32 = mybir.dt.uint32
U16 = mybir.dt.uint16
U8 = mybir.dt.uint8
FP8X4 = mybir.dt.float8_e4m3fn_x4
FP4X4 = mybir.dt.float4_e2m1fn_x4
SILU = mybir.ActivationFunctionType.Silu
MULT = mybir.AluOpType.mult

P = 128
PACK = 4
HALF = V // 2
X_FIRST = 512
Z_VECTOR = (64, 72)


def interleave(copy, dst, src):
    copy(out=dst.rearrange("p (c i) t -> p c t i", i=2), in_=src.rearrange("p t (c i) -> p c t i", i=2))


def quantize(nc, codes, scales, grouped):
    nc.vector.quantize_mx(out=codes.bitcast(FP8X4), scales=scales, in_=grouped.rearrange("p c t -> p (c t)"))


def tile_picked_tokmixl_silu_po_kernel(
    tc, x_words, x_scales, wa, gt, w1_words, w1_scales, offs, fl, out_0, out_1, out_2
):
    nc = tc.nc
    with ExitStack() as ctx:
        sb = ctx.enter_context(tc.tile_pool(name="sb", bufs=1))
        shared = ctx.enter_context(tc.tile_pool(name="shared", bufs=1))
        psum = ctx.enter_context(tc.psum_pool(name="psum", bufs=1))

        offs_sb = sb.tile([P, S // 16], U16, name="offs_sb")
        fl_sb = sb.tile([P, V // 16], U16, name="fl_sb")
        xw = shared.tile([P, T], I32, name="xw", align_bytes=64, offset=0)
        xs = sb.tile([P, T], U8, name="xs", align_bytes=64)
        wa_raw = [
            sb.tile([P, PACK, 256], F32, name="wa_raw0", align_bytes=64),
            shared.tile([P, PACK, 256], F32, name="wa_raw1", align_bytes=64, offset=8192 + 1024),
        ]
        w1w = sb.tile([P, 2 * N], U8, name="w1w", align_bytes=64)
        w1s = sb.tile([P, N], U8, name="w1s", align_bytes=64)
        gt_sb = sb.tile([P, PACK], F32, name="gt_sb", align_bytes=64)
        warm_in = sb.tile([P, 1], F32, name="warm_in")
        warm_out = sb.tile([P, 1], F32, name="warm_out")

        wa_rows = wa.rearrange("(p j) c -> p j c", j=PACK)

        nc.vector.memset(xs[:].bitcast(I32), 0)
        nc.vector.memset(warm_in[:], 0.0)
        nc.vector.memset(w1s[:].bitcast(I32), 0)

        x_rows = x_words[0].rearrange("p n t -> p (n t)").bitcast(I32)
        nc.sync.dma_start(out=xw[:, 0:X_FIRST], in_=x_rows[:, 0:X_FIRST])
        nc.sync.dma_start(offs_sb[:], offs)
        nc.sync.dma_start(out=gt_sb[:], in_=gt.rearrange("(p t) o -> p (t o)", t=PACK))
        for q in range(4):
            nc.sync.dma_start(
                out=xs[q:P:32, :].bitcast(I32), in_=x_scales[0, q:16:4, :].bitcast(I32)
            )
        nc.sync.dma_start(out=xw[:, X_FIRST:T], in_=x_rows[:, X_FIRST:T])
        for u in range(2):
            nc.sync.dma_start(out=wa_raw[u][:], in_=wa_rows[:, :, 256 * u : 256 * (u + 1)])
        nc.sync.dma_start(out=w1w[:].bitcast(I32), in_=w1_words[0].bitcast(I32))
        for q in range(4):
            nc.sync.dma_start(
                out=w1s[q:P:32, :].bitcast(I32), in_=w1_scales[0, q:16:4, :].bitcast(I32)
            )
        nc.sync.dma_start(fl_sb[:], fl)

        nc.scalar.activation(out=warm_out[:], in_=warm_in[:], func=SILU)

        gtb = sb.tile([P, 3, V], F32, name="gtb", align_bytes=64)
        gth = sb.tile([P, HALF], F32, name="gth", align_bytes=64)
        nc.scalar.copy(out=gtb[:], in_=gt_sb[:, 0:3].unsqueeze(2).to_broadcast([P, 3, V]))
        nc.scalar.copy(out=gth[:], in_=gt_sb[:, 3:4].to_broadcast([P, HALF]))

        g = sb.tile([P, PACK, V], F32, name="g", align_bytes=64)

        xsg = [sb.tile([P, S // 2], U8, name="xsg%d" % a, align_bytes=64) for a in range(2)]
        xsd = sb.tile([P, S], U8, name="xsd", align_bytes=64)
        for a in range(2):
            nc.vector.tensor_copy(out=xsg[a][:], in_=xs[:].indirect(offs_sb[:, 16 * a : 16 * (a + 1)]))
        for a in range(2):
            nc.vector.tensor_copy(
                out=xsd[:].rearrange("p (t s) -> p t s", t=PACK)[:, :, 64 * a : 64 * (a + 1)],
                in_=xsg[a][:].rearrange("p (s t) -> p t s", t=PACK),
            )
        xg = sb.tile([P, S], I32, name="xg", align_bytes=64)
        nc.vector.tensor_copy(
            out=xg[:].bitcast(U32).rearrange("p (t s) -> p s t", t=PACK),
            in_=xw[:].bitcast(U32).indirect(offs_sb[:]),
        )

        wb = [
            sb.tile([P, 128, PACK], BF16, name="wb0", align_bytes=64),
            sb.tile([P, 128, PACK], BF16, name="wb1", align_bytes=64),
            sb.tile([P, 128, PACK], BF16, name="wb2", align_bytes=64),
            shared.tile([P, 128, PACK], BF16, name="wb3", align_bytes=64, offset=1024),
        ]
        wc = shared.tile([P, H], I32, name="wc", align_bytes=64, offset=3072)
        ws = shared.tile([P, H], U8, name="ws", align_bytes=64, offset=5120)
        for u in range(2):
            share = (128, 96)[u]
            interleave(nc.scalar.copy, wb[2 * u][:, 0:share, :], wa_raw[u][:, :, 0:share])
            interleave(nc.vector.tensor_copy, wb[2 * u + 1][:], wa_raw[u][:, :, 128:256])
            if share < 128:
                interleave(nc.vector.tensor_copy, wb[2 * u][:, share:128, :], wa_raw[u][:, :, share:128])
            for e in (1, 0):
                cols = slice(256 * u + 128 * e, 256 * u + 128 * (e + 1))
                quantize(nc, wc[:, cols], ws[:, cols], wb[2 * u + e][:])

        w1sd = shared.tile([P, N], U8, name="w1sd", align_bytes=64, offset=1024 + 64)
        nc.vector.tensor_copy(
            out=w1sd[:].rearrange("p (t s) -> p t s", t=PACK), in_=w1s[:].rearrange("p (s t) -> p t s", t=PACK)
        )

        act = [shared.tile([P, H], F32, name="act%d" % t, align_bytes=64, offset=8192 + 2048 * t) for t in range(PACK)]

        def project(out, t, cols):
            nc.tensor.matmul_mx(
                out=out,
                lhsT=xg[:, P * t : P * (t + 1)].bitcast(FP8X4),
                lhsT_scale=xsd[:, P * t : P * (t + 1)],
                rhs=wc[:, cols].bitcast(FP8X4),
                rhs_scale=ws[:, cols],
                start=True,
                stop=True,
            )

        def activate(t, cols, y):
            nc.scalar.activation(out=act[t][:, cols], in_=y, func=SILU)

        early = [psum.tile([P, 256], F32, name="early%d" % t, tag="bank%d" % t) for t in range(2)]
        for cols in (slice(128, 256), slice(0, 128)):
            for t in range(2):
                project(early[t][:, cols], t, cols)
        for t in range(2):
            activate(t, slice(0, 256), early[t][:])
        whole = psum.tile([P, H], F32, name="whole", tag="bank4")
        project(whole[:, 0:256], 2, slice(0, 256))
        for t, cols, bank in ((0, slice(384, 512), 5), (0, slice(256, 384), 2), (1, slice(256, 512), 3)):
            y = psum.tile([P, cols.stop - cols.start], F32, name="y", tag="bank%d" % bank)
            project(y[:], t, cols)
            activate(t, cols, y[:])
        project(whole[:, 256:512], 2, slice(256, 512))
        activate(2, slice(0, 512), whole[:])
        last = psum.tile([P, H], F32, name="last", tag="bank1")
        project(last[:], 3, slice(0, 512))
        activate(3, slice(0, 512), last[:])

        w1d = shared.tile([P, 2 * N], U8, name="w1d", align_bytes=64, offset=3072)
        nc.scalar.copy(
            out=w1d[:].bitcast(U16).rearrange("p (t s) -> p t s", t=PACK),
            in_=w1w[:].bitcast(U16).rearrange("p (s t) -> p t s", t=PACK),
        )

        for t in range(3):
            nc.vector.tensor_tensor(out=g[:, t, :], in0=act[t][:].indirect(fl_sb[:]), in1=gtb[:, t, :], op=MULT)
        for h in range(2):
            nc.vector.tensor_tensor(
                out=g[:, 3, HALF * h : HALF * (h + 1)],
                in0=act[3][:].indirect(fl_sb[:, 8 * h : 8 * h + 8]),
                in1=gth[:],
                op=MULT,
            )

        zb = [sb.tile([P, HALF, PACK], BF16, name="zb%d" % h, align_bytes=64) for h in range(2)]
        zc = [sb.tile([P, HALF], I32, name="zc%d" % h, align_bytes=64) for h in range(2)]
        zs = [sb.tile([P, HALF], U8, name="zs%d" % h, align_bytes=64) for h in range(2)]
        for h in range(2):
            split = HALF * h + Z_VECTOR[h]
            interleave(nc.vector.tensor_copy, zb[h][:, 0 : Z_VECTOR[h], :], g[:, :, HALF * h : split])
            interleave(nc.scalar.copy, zb[h][:, Z_VECTOR[h] : HALF, :], g[:, :, split : HALF * (h + 1)])
        for h in range(2):
            quantize(nc, zc[h][:], zs[h][:], zb[h][:])

        o32 = sb.tile([P, PACK, V], F32, name="o32", align_bytes=64)
        ob = [sb.tile([P, HALF, PACK], BF16, name="ob%d" % h, align_bytes=64) for h in range(2)]
        oc = sb.tile([P, V], I32, name="oc", align_bytes=64)
        osc = sb.tile([P, V], U8, name="osc", align_bytes=64)
        out_rows = out_0.rearrange("(p t) v -> p t v", t=PACK)
        out_words = out_1[0].rearrange("p n t -> p (n t)").bitcast(I32)
        for h in range(2):
            cols = slice(HALF * h, HALF * (h + 1))
            groups = ((0, 1), (2, 3)) if h == 0 else ((0, 1), (2,), (3,))
            for slots in groups:
                acc = psum.tile([P, len(slots), HALF], F32, name="acc", tag="bank%d" % ((5 + 3 * h + slots[0]) % 8))
                for e, t in enumerate(slots):
                    nc.tensor.matmul_mx(
                        out=acc[:, e, :],
                        lhsT=w1d[:, 2 * P * t : 2 * P * (t + 1)].bitcast(FP4X4),
                        lhsT_scale=w1sd[:, P * t : P * (t + 1)],
                        rhs=zc[h][:].bitcast(FP8X4),
                        rhs_scale=zs[h][:],
                        start=True,
                        stop=True,
                    )
                if slots == (3,):
                    for c in (0, 64):
                        nc.scalar.copy(out=o32[:, 3, HALF + c : HALF + c + 64], in_=acc[:, 0, c : c + 64])
                else:
                    nc.scalar.copy(out=o32[:, slots[0] : slots[-1] + 1, cols], in_=acc[:])
            nc.sync.dma_start(out=out_rows[:, :, cols], in_=o32[:, :, cols])
            if h == 0:
                interleave(nc.vector.tensor_copy, ob[h][:], o32[:, :, cols])
                quantize(nc, oc[:, cols], osc[:, cols], ob[h][:])
            else:
                for c, copy in ((0, nc.vector.tensor_copy), (64, nc.scalar.copy)):
                    interleave(copy, ob[h][:, c : c + 64, :], o32[:, :, HALF + c : HALF + c + 64])
                for c in (0, 64):
                    part = slice(HALF + c, HALF + c + 64)
                    quantize(nc, oc[:, part], osc[:, part], ob[h][:, c : c + 64, :])
            nc.sync.dma_start(out=out_words[:, cols], in_=oc[:, cols])
        for q in range(4):
            eng = nc.scalar if q < 2 else nc.sync
            eng.dma_start(
                out=out_2[0, q:16:4, :].bitcast(I32), in_=osc[q:P:32, :].bitcast(I32)
            )
